import numpy as np
import ml_dtypes


def mxq(x, axis, fmt="e4m3"):
    dtype, down = {"e4m3": (ml_dtypes.float8_e4m3fn, 7), "e5m2": (ml_dtypes.float8_e5m2, 14)}[fmt]
    v = np.moveaxis(np.asarray(x, np.float32).astype(ml_dtypes.bfloat16).astype(np.float64), axis, -1)
    blocks = v.reshape(v.shape[:-1] + (-1, 32))
    amax = np.abs(blocks).max(-1, keepdims=True)
    byte = np.maximum(np.where(amax > 0, np.frexp(amax)[1] - 1 + 127, 0) - down, 1)
    scale = np.exp2(byte - 127.0)
    codes = (blocks / scale).astype(np.float32).astype(dtype).astype(np.float64)
    return np.moveaxis((codes * scale).reshape(v.shape), -1, axis)


WIDE = False


def mx_kscale(k):
    if not WIDE:
        return np.ones(k)
    levels = np.array([10, -10, 5, -5, 0])
    if k % 512:
        return np.exp2(np.random.permutation(np.resize(levels, k // 32))).repeat(32)
    a = np.empty((k // 512, 16))
    for p in range(k // 512):
        a[p, :8] = np.random.permutation(np.resize(levels, 8))
        for g in range(8):
            far = levels[np.abs(levels - a[p, g]) >= 10]
            a[p, g + 8] = far[np.random.randint(len(far))]
    return np.exp2(a.ravel()).repeat(32)


def f64(x):
    return np.asarray(x).astype(np.float64)


def striped(idx):
    return np.tile(np.asarray(idx).reshape(-1, 16).T, (8, 1)).astype(np.uint16)


def unstriped(offs):
    return offs[:16].T.reshape(-1).astype(np.int64)


E2M1 = np.array([0.0, 0.5, 1.0, 1.5, 2.0, 3.0, 4.0, 6.0, -0.0, -0.5, -1.0, -1.5, -2.0, -3.0, -4.0, -6.0])


def pack_weight(w, fmt):
    k, n = w.shape
    w = f64(np.asarray(w, np.float32).astype(ml_dtypes.bfloat16)).reshape(k // 32, 32, n)
    amax = np.abs(w).max(1)
    if fmt == "e4m3":
        byte = np.frexp(amax)[1] - 1 + 127 - 7
    else:
        mant, ex = np.frexp(amax / 6.0)
        byte = np.where(mant > 0.5, ex, ex - 1) + 127
    byte = np.clip(np.where(amax > 0, byte, 1), 1, 254)
    scaled = (w * np.exp2(127.0 - byte)[:, None, :]).reshape(k, n).astype(np.float32)
    by_word = np.ascontiguousarray(scaled.reshape(k // 512, 128, 4, n).transpose(0, 1, 3, 2))
    if fmt == "e4m3":
        words = by_word.astype(ml_dtypes.float8_e4m3fn).view(np.uint8)
    else:
        c = by_word.astype(ml_dtypes.float4_e2m1fn).view(np.uint8) & 0xF
        words = (c[..., 0::2] | (c[..., 1::2] << 4)).reshape(k // 512, 128, 2 * n)
    return np.ascontiguousarray(words), np.ascontiguousarray(byte.astype(np.uint8).reshape(k // 512, 16, n))


def unpack_weight(words, scales, fmt):
    g, _, n = scales.shape
    words = np.ascontiguousarray(words).reshape(g, 128, n, -1)
    if fmt == "e4m3":
        vals = words.view(ml_dtypes.float8_e4m3fn).astype(np.float64)
    else:
        nib = np.empty((g, 128, n, 4), np.uint8)
        nib[..., 0::2] = words & 0xF
        nib[..., 1::2] = words >> 4
        vals = E2M1[nib]
    vals = vals * np.repeat(np.exp2(scales.astype(np.float64) - 127.0), 8, axis=1)[..., None]
    return vals.transpose(0, 1, 3, 2).reshape(g * 512, n)


K, T, I, J, L, N = 512, 1024, 512, 256, 512, 512


def setup_inputs():
    n = np.random.standard_normal
    idx = np.random.permutation(T)[:I]
    idx2 = np.random.randint(0, I, J)
    fk = mx_kscale(K)
    fl = mx_kscale(L)
    xtp = pack_weight(n((K, T)) / fk[:, None], "e2m1")
    wp = pack_weight(n((K, N)) * 1 / np.sqrt(K) * fk[:, None], "e4m3")
    wrp = pack_weight(n((L, N)) * 1 / np.sqrt(L) * fl[:, None], "e4m3")
    return {
        "xt_words": xtp[0],
        "xt_scales": xtp[1],
        "w_words": wp[0],
        "w_scales": wp[1],
        "rq": (n((L, J)) / fl[:, None]).astype(np.float32),
        "wr_words": wrp[0],
        "wr_scales": wrp[1],
        "di": (np.random.uniform(0.5, 2.0, (1, I))).astype(np.float32),
        "offs": striped(idx),
        "offs2": striped(idx2),
    }


def reference(xt_words, xt_scales, w_words, w_scales, rq, wr_words, wr_scales, di, offs, offs2):
    idx = unstriped(offs)
    idx2 = unstriped(offs2)
    xtu = unpack_weight(xt_words, xt_scales, "e2m1")
    wu = unpack_weight(w_words, w_scales, "e4m3")
    wru = unpack_weight(wr_words, wr_scales, "e4m3")
    z = wu.T @ xtu
    dz = z[:, idx] * f64(di)
    rqq = mxq(f64(rq), 0, "e4m3")
    r = wru.T @ rqq
    y = np.tanh(dz[:, idx2]) + r
    return y

@@ -1,0 +1,177 @@
+from contextlib import ExitStack
+
+import concourse.mybir as mybir
+
+K, T, I, J, L, N = 512, 1024, 512, 256, 512, 512
+FLOPS = 2 * K * N * T + 2 * L * N * J
+
+F32 = mybir.dt.float32
+BF16 = mybir.dt.bfloat16
+I32 = mybir.dt.int32
+U32 = mybir.dt.uint32
+U16 = mybir.dt.uint16
+U8 = mybir.dt.uint8
+FP8X4 = mybir.dt.float8_e4m3fn_x4
+FP4X4 = mybir.dt.float4_e2m1fn_x4
+ACT = mybir.ActivationFunctionType
+ALU = mybir.AluOpType
+
+P = 128
+PACK = 4
+BANK = 512
+BLOCKS = N // P
+
+
+def load_scale_rows(queue, plane, scales, q):
+    queue.dma_start(out=plane[32 * q : 32 * q + 4, :].bitcast(I32), in_=scales[0, 4 * q : 4 * q + 4, :].bitcast(I32))
+
+
+def tile_list_link_of_link_kernel(tc, xt_words, xt_scales, w_words, w_scales, rq, wr_words, wr_scales, di, offs, offs2, out):
+    nc = tc.nc
+    with ExitStack() as ctx:
+        keep = ctx.enter_context(tc.tile_pool(name="keep", bufs=1))
+        psum = ctx.enter_context(tc.psum_pool(name="psum", bufs=1))
+
+        x_plane = keep.tile([P, T], U8, align_bytes=64)
+        w_plane = keep.tile([P, N], U8, align_bytes=64)
+        wr_plane = keep.tile([P, N], U8, align_bytes=64)
+        x_codes = keep.tile([P, 2 * T], U8, align_bytes=64)
+        w_codes = keep.tile([P, N], U32, align_bytes=64)
+        wr_codes = keep.tile([P, N], U32, align_bytes=64)
+        rq_raw = keep.tile([P, PACK, J], F32)
+        rq_bf = keep.tile([P, J, PACK], BF16, align_bytes=64, name="dz0")
+        rq_codes = keep.tile([P, J], U32, align_bytes=64)
+        rq_plane = keep.tile([P, J], U8, align_bytes=64)
+        list1 = keep.tile([P, I // 16], U16)
+        list2 = keep.tile([P, J // 16], U16)
+        di_cols = keep.tile([P, PACK], F32)
+        di_rows = keep.tile([P, I], F32)
+        ident = keep.tile([P, P], F32)
+        diag = keep.tile([P, P], I32)
+        warm = keep.tile([P, 1], F32)
+
+        nc.vector.memset(warm[:], 0.0)
+
+        nc.gpsimd.iota(diag[:], pattern=[[-1, P]], base=0, channel_multiplier=1)
+        nc.vector.tensor_scalar(out=ident[:], in0=diag[:], scalar1=0.0, scalar2=None, op0=ALU.is_equal)
+        nc.gpsimd.dma_start(out=rq_raw[:].rearrange("p t j -> p (t j)"), in_=rq.rearrange("(p t) j -> p (t j)", t=PACK))
+        load_scale_rows(nc.sync, x_plane, xt_scales, 0)
+        load_scale_rows(nc.sync, w_plane, w_scales, 0)
+        load_scale_rows(nc.sync, x_plane, xt_scales, 1)
+        nc.sync.dma_start(out=di_cols[:], in_=di.rearrange("o (p c) -> (o p) c", c=PACK))
+        nc.sync.dma_start(out=x_codes[:].bitcast(I32), in_=xt_words[0].bitcast(I32))
+        nc.sync.dma_start(out=w_codes[:].bitcast(I32), in_=w_words[0].rearrange("p n t -> p (n t)").bitcast(I32))
+        load_scale_rows(nc.sync, w_plane, w_scales, 1)
+        load_scale_rows(nc.sync, w_plane, w_scales, 2)
+        load_scale_rows(nc.sync, w_plane, w_scales, 3)
+        load_scale_rows(nc.sync, x_plane, xt_scales, 2)
+        load_scale_rows(nc.sync, x_plane, xt_scales, 3)
+        nc.sync.dma_start(list1[:], offs)
+        nc.sync.dma_start(out=wr_codes[:].bitcast(I32), in_=wr_words[0].rearrange("p n t -> p (n t)").bitcast(I32))
+        nc.sync.dma_start(list2[:], offs2)
+        for q in range(4):
+            load_scale_rows(nc.sync, wr_plane, wr_scales, q)
+
+        nc.scalar.activation(out=warm[:], in_=warm[:], func=ACT.Sigmoid)
+
+        z = [keep.tile([P, T], F32, name="z%d" % b) for b in range(BLOCKS)]
+        dz = []
+        sg = [keep.tile([P, J], F32, name="sg%d" % b) for b in range(BLOCKS)]
+        y = [keep.tile([P, J], F32, name="y%d" % b) for b in range(BLOCKS)]
+        r_less_one = keep.tile([P, J], F32)
+        r_acc = []
+
+        banks = [0]
+
+        def make_z(b):
+            cols = slice(b * P, (b + 1) * P)
+            width = 256 if b == 0 else BANK
+            for lo in range(0, T, width):
+                hi = lo + width
+                acc = psum.tile([P, hi - lo], F32, name="z_acc%d" % (banks[0] % 6))
+                banks[0] = banks[0] + 1
+                nc.tensor.matmul_mx(
+                    out=acc[:],
+                    lhsT=w_codes[:, cols].bitcast(FP8X4),
+                    lhsT_scale=w_plane[:, cols],
+                    rhs=x_codes[:, 2 * lo : 2 * hi].bitcast(FP4X4),
+                    rhs_scale=x_plane[:, lo:hi],
+                    start=True,
+                    stop=True,
+                )
+                nc.scalar.copy(out=z[b][:, lo:hi], in_=acc[:])
+
+        def spread_di():
+            acc = psum.tile([P, PACK, P], F32, name="z_acc0")
+            for c in range(PACK):
+                nc.tensor.transpose(acc[:, c, :], di_cols[:, c : c + 1].to_broadcast([P, P]), ident[:])
+            nc.scalar.copy(out=di_rows[:].rearrange("p (q c) -> p q c", c=PACK), in_=acc[:].rearrange("p c q -> p q c"))
+
+        def quantize_rq():
+            nc.vector.tensor_copy(
+                out=rq_bf[:].rearrange("p (c i) t -> p c t i", i=4),
+                in_=rq_raw[:].rearrange("p t (c i) -> p c t i", i=4),
+            )
+            nc.vector.quantize_mx(out=rq_codes[:].bitcast(FP8X4), scales=rq_plane[:], in_=rq_bf[:].rearrange("p j t -> p (j t)"))
+
+        def make_r(h):
+            acc = psum.tile([P, 2 * J], F32, name="r_acc%d" % h)
+            r_acc.append(acc)
+            for u in range(2):
+                cols = slice((2 * h + u) * P, (2 * h + u + 1) * P)
+                nc.tensor.matmul_mx(
+                    out=acc[:, u * J : (u + 1) * J],
+                    lhsT=wr_codes[:, cols].bitcast(FP8X4),
+                    lhsT_scale=wr_plane[:, cols],
+                    rhs=rq_codes[:].bitcast(FP8X4),
+                    rhs_scale=rq_plane[:],
+                    start=True,
+                    stop=True,
+                )
+
+        def look_up_z(b):
+            dz.append(keep.tile([P, I], F32, align_bytes=64, name="dz%d" % b))
+            nc.vector.tensor_tensor(dz[b][:], z[b][:].indirect(list1[:]), di_rows[:], ALU.mult)
+
+        def look_up_dz(b):
+            nc.scalar.activation(out=sg[b][:], in_=dz[b][:].indirect(list2[:]), func=ACT.Sigmoid, scale=2.0)
+
+        def r_block(b):
+            return r_acc[b // 2][:, (b % 2) * J : (b % 2 + 1) * J]
+
+        def to_tanh(b):
+            nc.vector.tensor_scalar(out=sg[b][:], in0=sg[b][:], scalar1=2.0, scalar2=-1.0, op0=ALU.mult, op1=ALU.add)
+
+        def store(b):
+            nc.sync.dma_start(out=out[b * P : (b + 1) * P, :], in_=y[b][:])
+
+        def finish(b):
+            nc.vector.tensor_tensor(y[b][:], sg[b][:], r_block(b), ALU.add)
+            store(b)
+
+        last = BLOCKS - 1
+        spread_di()
+        quantize_rq()
+        make_z(0)
+        make_z(1)
+        look_up_z(0)
+        make_z(2)
+        look_up_z(1)
+        look_up_dz(0)
+        make_z(3)
+        make_r(0)
+        make_r(1)
+        to_tanh(0)
+        look_up_z(2)
+        look_up_dz(1)
+        finish(0)
+        nc.scalar.activation(out=r_less_one[:], in_=r_block(last), func=ACT.Identity, bias=-1.0)
+        to_tanh(1)
+        look_up_z(3)
+        look_up_dz(2)
+        finish(1)
+        to_tanh(2)
+        look_up_dz(3)
+        finish(2)
+        nc.vector.scalar_tensor_tensor(out=y[last][:], in0=sg[last][:], scalar=2.0, in1=r_less_one[:], op0=ALU.mult, op1=ALU.add)
+        store(last)

@@ -1,6 +1,7 @@
 from contextlib import ExitStack
 
 import concourse.mybir as mybir
+from concourse.masks import make_identity
 
 K, T, I, J, L, N = 512, 1024, 512, 256, 512, 512
 FLOPS = 2 * K * N * T + 2 * L * N * J
@@ -36,7 +37,8 @@ def tile_list_link_of_link_kernel(tc, xt_words, xt_scales, w_words, w_scales, rq
         w_plane = keep.tile([P, N], U8, align_bytes=64)
         wr_plane = keep.tile([P, N], U8, align_bytes=64)
         x_codes = keep.tile([P, 2 * T], U8, align_bytes=64)
-        w_codes = keep.tile([P, N], U32, align_bytes=64)
+        w_first = keep.tile([P, P], U32, align_bytes=64)
+        w_rest = keep.tile([P, N - P], U32, align_bytes=64)
         wr_codes = keep.tile([P, N], U32, align_bytes=64)
         rq_raw = keep.tile([P, PACK, J], F32)
         rq_bf = keep.tile([P, J, PACK], BF16, align_bytes=64, name="dz0")
@@ -47,28 +49,25 @@ def tile_list_link_of_link_kernel(tc, xt_words, xt_scales, w_words, w_scales, rq
         di_cols = keep.tile([P, PACK], F32)
         di_rows = keep.tile([P, I], F32)
         ident = keep.tile([P, P], F32)
-        diag = keep.tile([P, P], I32)
         warm = keep.tile([P, 1], F32)
 
         nc.vector.memset(warm[:], 0.0)
 
-        nc.gpsimd.iota(diag[:], pattern=[[-1, P]], base=0, channel_multiplier=1)
-        nc.vector.tensor_scalar(out=ident[:], in0=diag[:], scalar1=0.0, scalar2=None, op0=ALU.is_equal)
-        nc.gpsimd.dma_start(out=rq_raw[:].rearrange("p t j -> p (t j)"), in_=rq.rearrange("(p t) j -> p (t j)", t=PACK))
-        load_scale_rows(nc.sync, x_plane, xt_scales, 0)
-        load_scale_rows(nc.sync, w_plane, w_scales, 0)
-        load_scale_rows(nc.sync, x_plane, xt_scales, 1)
+        make_identity(nc, ident[:])
+        w_rows = w_words[0].rearrange("p n t -> p (n t)").bitcast(I32)
         nc.sync.dma_start(out=di_cols[:], in_=di.rearrange("o (p c) -> (o p) c", c=PACK))
-        nc.sync.dma_start(out=x_codes[:].bitcast(I32), in_=xt_words[0].bitcast(I32))
-        nc.sync.dma_start(out=w_codes[:].bitcast(I32), in_=w_words[0].rearrange("p n t -> p (n t)").bitcast(I32))
-        load_scale_rows(nc.sync, w_plane, w_scales, 1)
-        load_scale_rows(nc.sync, w_plane, w_scales, 2)
-        load_scale_rows(nc.sync, w_plane, w_scales, 3)
-        load_scale_rows(nc.sync, x_plane, xt_scales, 2)
+        for q in range(3):
+            load_scale_rows(nc.sync, x_plane, xt_scales, q)
+        nc.sync.dma_start(out=rq_raw[:].rearrange("p t j -> p (t j)"), in_=rq.rearrange("(p t) j -> p (t j)", t=PACK))
         load_scale_rows(nc.sync, x_plane, xt_scales, 3)
+        nc.sync.dma_start(out=x_codes[:].bitcast(I32), in_=xt_words[0].bitcast(I32))
+        nc.sync.dma_start(out=w_first[:].bitcast(I32), in_=w_rows[:, 0:P])
+        for q in range(4):
+            load_scale_rows(nc.sync, w_plane, w_scales, q)
+        nc.sync.dma_start(out=w_rest[:].bitcast(I32), in_=w_rows[:, P:N])
         nc.sync.dma_start(list1[:], offs)
-        nc.sync.dma_start(out=wr_codes[:].bitcast(I32), in_=wr_words[0].rearrange("p n t -> p (n t)").bitcast(I32))
         nc.sync.dma_start(list2[:], offs2)
+        nc.sync.dma_start(out=wr_codes[:].bitcast(I32), in_=wr_words[0].rearrange("p n t -> p (n t)").bitcast(I32))
         for q in range(4):
             load_scale_rows(nc.sync, wr_plane, wr_scales, q)
 
@@ -76,8 +75,8 @@ def tile_list_link_of_link_kernel(tc, xt_words, xt_scales, w_words, w_scales, rq
 
         z = [keep.tile([P, T], F32, name="z%d" % b) for b in range(BLOCKS)]
         dz = []
-        sg = [keep.tile([P, J], F32, name="sg%d" % b) for b in range(BLOCKS)]
-        y = [keep.tile([P, J], F32, name="y%d" % b) for b in range(BLOCKS)]
+        sg = keep.tile([P, BLOCKS * J], F32)
+        y = keep.tile([P, BLOCKS * J], F32)
         r_less_one = keep.tile([P, J], F32)
         r_acc = []
 
@@ -92,17 +91,20 @@ def tile_list_link_of_link_kernel(tc, xt_words, xt_scales, w_words, w_scales, rq
                 banks[0] = banks[0] + 1
                 nc.tensor.matmul_mx(
                     out=acc[:],
-                    lhsT=w_codes[:, cols].bitcast(FP8X4),
+                    lhsT=(w_first[:] if b == 0 else w_rest[:, (b - 1) * P : b * P]).bitcast(FP8X4),
                     lhsT_scale=w_plane[:, cols],
                     rhs=x_codes[:, 2 * lo : 2 * hi].bitcast(FP4X4),
                     rhs_scale=x_plane[:, lo:hi],
                     start=True,
                     stop=True,
                 )
-                nc.scalar.copy(out=z[b][:, lo:hi], in_=acc[:])
+                if b == 0 and lo % BANK == 0:
+                    nc.vector.tensor_copy(out=z[b][:, lo:hi], in_=acc[:])
+                else:
+                    nc.scalar.copy(out=z[b][:, lo:hi], in_=acc[:])
 
         def spread_di():
-            acc = psum.tile([P, PACK, P], F32, name="z_acc0")
+            acc = psum.tile([P, PACK, P], F32, name="r_acc1")
             for c in range(PACK):
                 nc.tensor.transpose(acc[:, c, :], di_cols[:, c : c + 1].to_broadcast([P, P]), ident[:])
             nc.scalar.copy(out=di_rows[:].rearrange("p (q c) -> p q c", c=PACK), in_=acc[:].rearrange("p c q -> p q c"))
@@ -134,19 +136,21 @@ def tile_list_link_of_link_kernel(tc, xt_words, xt_scales, w_words, w_scales, rq
             nc.vector.tensor_tensor(dz[b][:], z[b][:].indirect(list1[:]), di_rows[:], ALU.mult)
 
         def look_up_dz(b):
-            nc.scalar.activation(out=sg[b][:], in_=dz[b][:].indirect(list2[:]), func=ACT.Sigmoid, scale=2.0)
+            nc.scalar.activation(out=sg[:, b * J : (b + 1) * J], in_=dz[b][:].indirect(list2[:]), func=ACT.Sigmoid, scale=2.0)
 
         def r_block(b):
             return r_acc[b // 2][:, (b % 2) * J : (b % 2 + 1) * J]
 
         def to_tanh(b):
-            nc.vector.tensor_scalar(out=sg[b][:], in0=sg[b][:], scalar1=2.0, scalar2=-1.0, op0=ALU.mult, op1=ALU.add)
+            cols = slice(b * J, (b + 1) * J)
+            nc.vector.tensor_scalar(out=sg[:, cols], in0=sg[:, cols], scalar1=2.0, scalar2=-1.0, op0=ALU.mult, op1=ALU.add)
 
         def store(b):
-            nc.sync.dma_start(out=out[b * P : (b + 1) * P, :], in_=y[b][:])
+            nc.sync.dma_start(out=out[b * P : (b + 1) * P, :], in_=y[:, b * J : (b + 1) * J])
 
         def finish(b):
-            nc.vector.tensor_tensor(y[b][:], sg[b][:], r_block(b), ALU.add)
+            cols = slice(b * J, (b + 1) * J)
+            nc.vector.tensor_tensor(y[:, cols], sg[:, cols], r_block(b), ALU.add)
             store(b)
 
         last = BLOCKS - 1
@@ -157,21 +161,21 @@ def tile_list_link_of_link_kernel(tc, xt_words, xt_scales, w_words, w_scales, rq
         look_up_z(0)
         make_z(2)
         look_up_z(1)
-        look_up_dz(0)
         make_z(3)
         make_r(0)
         make_r(1)
-        to_tanh(0)
+        look_up_dz(0)
         look_up_z(2)
         look_up_dz(1)
-        finish(0)
-        nc.scalar.activation(out=r_less_one[:], in_=r_block(last), func=ACT.Identity, bias=-1.0)
-        to_tanh(1)
         look_up_z(3)
         look_up_dz(2)
-        finish(1)
-        to_tanh(2)
+        nc.scalar.activation(out=r_less_one[:], in_=r_block(last), func=ACT.Identity, bias=-1.0)
         look_up_dz(3)
+        to_tanh(0)
+        to_tanh(1)
+        finish(0)
+        to_tanh(2)
+        finish(1)
         finish(2)
-        nc.vector.scalar_tensor_tensor(out=y[last][:], in0=sg[last][:], scalar=2.0, in1=r_less_one[:], op0=ALU.mult, op1=ALU.add)
+        nc.vector.scalar_tensor_tensor(out=y[:, last * J :], in0=sg[:, last * J :], scalar=2.0, in1=r_less_one[:], op0=ALU.mult, op1=ALU.add)
         store(last)

@@ -40,7 +40,7 @@ def tile_list_link_of_link_kernel(tc, xt_words, xt_scales, w_words, w_scales, rq
         w_first = keep.tile([P, P], U32, align_bytes=64)
         w_rest = keep.tile([P, N - P], U32, align_bytes=64)
         wr_codes = keep.tile([P, N], U32, align_bytes=64)
-        rq_raw = keep.tile([P, PACK, J], F32)
+        rq_raw = keep.tile([P, PACK * J], F32)
         rq_bf = keep.tile([P, J, PACK], BF16, align_bytes=64, name="dz0")
         rq_codes = keep.tile([P, J], U32, align_bytes=64)
         rq_plane = keep.tile([P, J], U8, align_bytes=64)
@@ -55,15 +55,16 @@ def tile_list_link_of_link_kernel(tc, xt_words, xt_scales, w_words, w_scales, rq
 
         make_identity(nc, ident[:])
         w_rows = w_words[0].rearrange("p n t -> p (n t)").bitcast(I32)
+        rq_rows = rq.rearrange("(p t) j -> p (t j)", t=PACK)
         nc.sync.dma_start(out=di_cols[:], in_=di.rearrange("o (p c) -> (o p) c", c=PACK))
-        for q in range(3):
+        for q in range(4):
             load_scale_rows(nc.sync, x_plane, xt_scales, q)
-        nc.sync.dma_start(out=rq_raw[:].rearrange("p t j -> p (t j)"), in_=rq.rearrange("(p t) j -> p (t j)", t=PACK))
-        load_scale_rows(nc.sync, x_plane, xt_scales, 3)
         nc.sync.dma_start(out=x_codes[:].bitcast(I32), in_=xt_words[0].bitcast(I32))
         nc.sync.dma_start(out=w_first[:].bitcast(I32), in_=w_rows[:, 0:P])
+        nc.sync.dma_start(out=rq_raw[:, 0 : 2 * J], in_=rq_rows[:, 0 : 2 * J])
         for q in range(4):
             load_scale_rows(nc.sync, w_plane, w_scales, q)
+        nc.sync.dma_start(out=rq_raw[:, 2 * J : 4 * J], in_=rq_rows[:, 2 * J : 4 * J])
         nc.sync.dma_start(out=w_rest[:].bitcast(I32), in_=w_rows[:, P:N])
         nc.sync.dma_start(list1[:], offs)
         nc.sync.dma_start(list2[:], offs2)
@@ -98,10 +99,7 @@ def tile_list_link_of_link_kernel(tc, xt_words, xt_scales, w_words, w_scales, rq
                     start=True,
                     stop=True,
                 )
-                if b == 0 and lo % BANK == 0:
-                    nc.vector.tensor_copy(out=z[b][:, lo:hi], in_=acc[:])
-                else:
-                    nc.scalar.copy(out=z[b][:, lo:hi], in_=acc[:])
+                nc.scalar.copy(out=z[b][:, lo:hi], in_=acc[:])
 
         def spread_di():
             acc = psum.tile([P, PACK, P], F32, name="r_acc1")
@@ -112,7 +110,7 @@ def tile_list_link_of_link_kernel(tc, xt_words, xt_scales, w_words, w_scales, rq
         def quantize_rq():
             nc.vector.tensor_copy(
                 out=rq_bf[:].rearrange("p (c i) t -> p c t i", i=4),
-                in_=rq_raw[:].rearrange("p t (c i) -> p c t i", i=4),
+                in_=rq_raw[:].rearrange("p (t c i) -> p c t i", t=PACK, i=4),
             )
             nc.vector.quantize_mx(out=rq_codes[:].bitcast(FP8X4), scales=rq_plane[:], in_=rq_bf[:].rearrange("p j t -> p (j t)"))
 
@@ -153,7 +151,6 @@ def tile_list_link_of_link_kernel(tc, xt_words, xt_scales, w_words, w_scales, rq
             nc.vector.tensor_tensor(y[:, cols], sg[:, cols], r_block(b), ALU.add)
             store(b)
 
-        last = BLOCKS - 1
         spread_di()
         quantize_rq()
         make_z(0)
@@ -168,9 +165,10 @@ def tile_list_link_of_link_kernel(tc, xt_words, xt_scales, w_words, w_scales, rq
         look_up_z(2)
         look_up_dz(1)
         look_up_z(3)
+        last = BLOCKS - 1
         look_up_dz(2)
-        nc.scalar.activation(out=r_less_one[:], in_=r_block(last), func=ACT.Identity, bias=-1.0)
         look_up_dz(3)
+        nc.vector.tensor_scalar(out=r_less_one[:], in0=r_block(last), scalar1=-1.0, scalar2=None, op0=ALU.add)
         to_tanh(0)
         to_tanh(1)
         finish(0)

from contextlib import ExitStack

import concourse.mybir as mybir
from concourse.masks import make_identity

K, T, I, J, L, N = 512, 1024, 512, 256, 512, 512
FLOPS = 2 * K * N * T + 2 * L * N * J

F32 = mybir.dt.float32
BF16 = mybir.dt.bfloat16
I32 = mybir.dt.int32
U32 = mybir.dt.uint32
U16 = mybir.dt.uint16
U8 = mybir.dt.uint8
FP8X4 = mybir.dt.float8_e4m3fn_x4
FP4X4 = mybir.dt.float4_e2m1fn_x4
ACT = mybir.ActivationFunctionType
ALU = mybir.AluOpType

P = 128
PACK = 4
BANK = 512
BLOCKS = N // P


def load_scale_rows(queue, plane, scales, q):
    queue.dma_start(out=plane[32 * q : 32 * q + 4, :].bitcast(I32), in_=scales[0, 4 * q : 4 * q + 4, :].bitcast(I32))


def tile_list_link_of_link_kernel(tc, xt_words, xt_scales, w_words, w_scales, rq, wr_words, wr_scales, di, offs, offs2, out):
    nc = tc.nc
    with ExitStack() as ctx:
        keep = ctx.enter_context(tc.tile_pool(name="keep", bufs=1))
        psum = ctx.enter_context(tc.psum_pool(name="psum", bufs=1))

        x_plane = keep.tile([P, T], U8, align_bytes=64)
        w_plane = keep.tile([P, N], U8, align_bytes=64)
        wr_plane = keep.tile([P, N], U8, align_bytes=64)
        x_codes = keep.tile([P, 2 * T], U8, align_bytes=64)
        w_first = keep.tile([P, P], U32, align_bytes=64)
        w_rest = keep.tile([P, N - P], U32, align_bytes=64)
        wr_codes = keep.tile([P, N], U32, align_bytes=64)
        rq_raw = keep.tile([P, PACK * J], F32)
        rq_bf = keep.tile([P, J, PACK], BF16, align_bytes=64, name="dz0")
        rq_codes = keep.tile([P, J], U32, align_bytes=64)
        rq_plane = keep.tile([P, J], U8, align_bytes=64)
        list1 = keep.tile([P, I // 16], U16)
        list2 = keep.tile([P, J // 16], U16)
        di_cols = keep.tile([P, PACK], F32)
        di_rows = keep.tile([P, I], F32)
        ident = keep.tile([P, P], F32)
        warm = keep.tile([P, 1], F32)

        nc.vector.memset(warm[:], 0.0)

        make_identity(nc, ident[:])
        w_rows = w_words[0].rearrange("p n t -> p (n t)").bitcast(I32)
        rq_rows = rq.rearrange("(p t) j -> p (t j)", t=PACK)
        nc.sync.dma_start(out=di_cols[:], in_=di.rearrange("o (p c) -> (o p) c", c=PACK))
        for q in range(4):
            load_scale_rows(nc.sync, x_plane, xt_scales, q)
        nc.sync.dma_start(out=x_codes[:].bitcast(I32), in_=xt_words[0].bitcast(I32))
        nc.sync.dma_start(out=w_first[:].bitcast(I32), in_=w_rows[:, 0:P])
        nc.sync.dma_start(out=rq_raw[:, 0 : 2 * J], in_=rq_rows[:, 0 : 2 * J])
        for q in range(4):
            load_scale_rows(nc.sync, w_plane, w_scales, q)
        nc.sync.dma_start(out=rq_raw[:, 2 * J : 4 * J], in_=rq_rows[:, 2 * J : 4 * J])
        nc.sync.dma_start(out=w_rest[:].bitcast(I32), in_=w_rows[:, P:N])
        nc.sync.dma_start(list1[:], offs)
        nc.sync.dma_start(list2[:], offs2)
        nc.sync.dma_start(out=wr_codes[:].bitcast(I32), in_=wr_words[0].rearrange("p n t -> p (n t)").bitcast(I32))
        for q in range(4):
            load_scale_rows(nc.sync, wr_plane, wr_scales, q)

        nc.scalar.activation(out=warm[:], in_=warm[:], func=ACT.Sigmoid)

        z = [keep.tile([P, T], F32, name="z%d" % b) for b in range(BLOCKS)]
        dz = []
        sg = keep.tile([P, BLOCKS * J], F32)
        y = keep.tile([P, BLOCKS * J], F32)
        r_less_one = keep.tile([P, J], F32)
        r_acc = []

        banks = [0]

        def make_z(b):
            cols = slice(b * P, (b + 1) * P)
            width = 256 if b == 0 else BANK
            for lo in range(0, T, width):
                hi = lo + width
                acc = psum.tile([P, hi - lo], F32, name="z_acc%d" % (banks[0] % 6))
                banks[0] = banks[0] + 1
                nc.tensor.matmul_mx(
                    out=acc[:],
                    lhsT=(w_first[:] if b == 0 else w_rest[:, (b - 1) * P : b * P]).bitcast(FP8X4),
                    lhsT_scale=w_plane[:, cols],
                    rhs=x_codes[:, 2 * lo : 2 * hi].bitcast(FP4X4),
                    rhs_scale=x_plane[:, lo:hi],
                    start=True,
                    stop=True,
                )
                nc.scalar.copy(out=z[b][:, lo:hi], in_=acc[:])

        def spread_di():
            acc = psum.tile([P, PACK, P], F32, name="r_acc1")
            for c in range(PACK):
                nc.tensor.transpose(acc[:, c, :], di_cols[:, c : c + 1].to_broadcast([P, P]), ident[:])
            nc.scalar.copy(out=di_rows[:].rearrange("p (q c) -> p q c", c=PACK), in_=acc[:].rearrange("p c q -> p q c"))

        def quantize_rq():
            nc.vector.tensor_copy(
                out=rq_bf[:].rearrange("p (c i) t -> p c t i", i=4),
                in_=rq_raw[:].rearrange("p (t c i) -> p c t i", t=PACK, i=4),
            )
            nc.vector.quantize_mx(out=rq_codes[:].bitcast(FP8X4), scales=rq_plane[:], in_=rq_bf[:].rearrange("p j t -> p (j t)"))

        def make_r(h):
            acc = psum.tile([P, 2 * J], F32, name="r_acc%d" % h)
            r_acc.append(acc)
            for u in range(2):
                cols = slice((2 * h + u) * P, (2 * h + u + 1) * P)
                nc.tensor.matmul_mx(
                    out=acc[:, u * J : (u + 1) * J],
                    lhsT=wr_codes[:, cols].bitcast(FP8X4),
                    lhsT_scale=wr_plane[:, cols],
                    rhs=rq_codes[:].bitcast(FP8X4),
                    rhs_scale=rq_plane[:],
                    start=True,
                    stop=True,
                )

        def look_up_z(b):
            dz.append(keep.tile([P, I], F32, align_bytes=64, name="dz%d" % b))
            nc.vector.tensor_tensor(dz[b][:], z[b][:].indirect(list1[:]), di_rows[:], ALU.mult)

        def look_up_dz(b):
            nc.scalar.activation(out=sg[:, b * J : (b + 1) * J], in_=dz[b][:].indirect(list2[:]), func=ACT.Sigmoid, scale=2.0)

        def r_block(b):
            return r_acc[b // 2][:, (b % 2) * J : (b % 2 + 1) * J]

        def to_tanh(b):
            cols = slice(b * J, (b + 1) * J)
            nc.vector.tensor_scalar(out=sg[:, cols], in0=sg[:, cols], scalar1=2.0, scalar2=-1.0, op0=ALU.mult, op1=ALU.add)

        def store(b):
            nc.sync.dma_start(out=out[b * P : (b + 1) * P, :], in_=y[:, b * J : (b + 1) * J])

        def finish(b):
            cols = slice(b * J, (b + 1) * J)
            nc.vector.tensor_tensor(y[:, cols], sg[:, cols], r_block(b), ALU.add)
            store(b)

        spread_di()
        quantize_rq()
        make_z(0)
        make_z(1)
        look_up_z(0)
        make_z(2)
        look_up_z(1)
        make_z(3)
        make_r(0)
        make_r(1)
        look_up_dz(0)
        look_up_z(2)
        look_up_dz(1)
        look_up_z(3)
        last = BLOCKS - 1
        look_up_dz(2)
        look_up_dz(3)
        nc.vector.tensor_scalar(out=r_less_one[:], in0=r_block(last), scalar1=-1.0, scalar2=None, op0=ALU.add)
        to_tanh(0)
        to_tanh(1)
        finish(0)
        to_tanh(2)
        finish(1)
        finish(2)
        nc.vector.scalar_tensor_tensor(out=y[:, last * J :], in0=sg[:, last * J :], scalar=2.0, in1=r_less_one[:], op0=ALU.mult, op1=ALU.add)
        store(last)
